import numpy as np
CORES = [1,9,17,25,102,110,118,126]
N = 8
ROOT = 5
def setup_inputs(rng):
    return {"x": rng.standard_normal((N, 128, 1024), dtype=np.float32)}
def reference(x):
    return {"y": np.broadcast_to(x[ROOT], x.shape)}

@@ -1,0 +1,42 @@
+from concourse.bass import DstId, RemoteDMATransfer
+
+SCRATCH = {
+    "land": ("sbuf", [128, 1024], "float32"),
+}
+SEMAPHORES = ["loaded", "read", "arrived", "stored"]
+
+ROOT = 110
+RELAY = 102
+ODD = [9, 25, 126]
+EVEN = [1, 17, 118]
+
+
+def _send(g, T, topo, dsts):
+    ids = []
+    for d in dsts:
+        rid, pid, _se = topo.addr(d)
+        ids.append(DstId(rid=rid, pnc=pid))
+    g.remote_dma_fused(
+        [RemoteDMATransfer(dst_ids=ids, dma_engine_mask=0xFF, remote_sem=T.sem.arrived,
+                           srcs=[T.land[:]], dsts=[T.land[:] for _d in dsts])],
+        local_sem=T.sem.read)
+    g.wait_ge(T.sem.read, 8)
+
+
+def rank_program(g, core, T, topo):
+    rank = T.rank_of(core)
+    if rank is None:
+        return
+    if core == ROOT:
+        g.sync.dma_start(T.y[:], T.x[:]).then_inc(T.sem.stored, 16)
+        g.dma_start(T.land[:], T.x[:]).then_inc(T.sem.loaded, 16)
+        g.wait_ge(T.sem.loaded, 16)
+        _send(g, T, topo, [RELAY] + ODD)
+        g.wait_ge(T.sem.stored, 16)
+        return
+    g.wait_ge(T.sem.arrived, 8)
+    g.sync.wait_ge(T.sem.arrived, 8)
+    g.sync.dma_start(T.y[:], T.land[:]).then_inc(T.sem.stored, 16)
+    if core == RELAY:
+        _send(g, T, topo, EVEN)
+    g.wait_ge(T.sem.stored, 16)

@@ -1,42 +1,79 @@
 from concourse.bass import DstId, RemoteDMATransfer
 
-SCRATCH = {
-    "land": ("sbuf", [128, 1024], "float32"),
-}
-SEMAPHORES = ["loaded", "read", "arrived", "stored"]
-
 ROOT = 110
-RELAY = 102
-ODD = [9, 25, 126]
-EVEN = [1, 17, 118]
+ROW = 1024
+PIECES = [
+    (15, 11), (7, 8),
+    (31, 11), (23, 8),
+    (127, 11), (119, 8),
+    (123, 11), (3, 8),
+    (11, 10), (19, 8),
+    (27, 10), (115, 8),
+    (98, 8), (99, 8),
+]
+NP = len(PIECES)
+START = [sum(r for (c, r) in PIECES[:k]) for k in range(NP)]
+
+SCRATCH = {"p%d" % k: ("dram", [128, PIECES[k][1] * ROW // 128], "float32") for k in range(NP)}
+SEMAPHORES = ["a%d" % k for k in range(NP)] + ["left", "stored"]
+
+OFF_CHIP = 0x00FF
+ON_CHIP = 0xFF00
 
 
-def _send(g, T, topo, dsts):
-    ids = []
-    for d in dsts:
-        rid, pid, _se = topo.addr(d)
-        ids.append(DstId(rid=rid, pnc=pid))
+def dst_id(topo, core):
+    rid, pid, sengine = topo.addr(core)
+    return DstId(rid=rid, pnc=pid)
+
+
+def rows_of(t, k):
+    return t[START[k]:START[k] + PIECES[k][1], :]
+
+
+def root_program(g, T, topo):
+    queues = [g.sync, g.scalar]
+    for k in range(NP):
+        queues[k % 2].dma_start(T["p%d" % k][:], rows_of(T.x, k)).then_inc(T.sem["a%d" % k], 16)
+    for k in range(NP):
+        rid, pid, sengine = topo.addr(PIECES[k][0])
+        g.wait_ge(T.sem["a%d" % k], 16)
+        g.remote_dma(T["p%d" % k][:], T["p%d" % k][:], T.sem["a%d" % k], T.sem.left, pid, rid, OFF_CHIP)
+    g.sync.wait_ge(T.sem.left, 8 * NP)
+    g.sync.dma_start(T.y[:], T.x[:]).then_inc(T.sem.stored, 16)
+    g.wait_ge(T.sem.stored, 16)
+
+
+def forwarder_program(g, core, k, T, topo):
+    buf = T["p%d" % k][:]
+    arrived = T.sem["a%d" % k]
+    far = [r for r in T.cores if r != ROOT and topo.chip(r) != topo.chip(core)]
+    near = [r for r in T.cores if topo.chip(r) == topo.chip(core)]
+    g.wait_ge(arrived, 8)
     g.remote_dma_fused(
-        [RemoteDMATransfer(dst_ids=ids, dma_engine_mask=0xFF, remote_sem=T.sem.arrived,
-                           srcs=[T.land[:]], dsts=[T.land[:] for _d in dsts])],
-        local_sem=T.sem.read)
-    g.wait_ge(T.sem.read, 8)
+        [RemoteDMATransfer(dst_ids=[dst_id(topo, r) for r in far], dma_engine_mask=OFF_CHIP, remote_sem=arrived,
+                           srcs=[buf], dsts=[buf for r in far]),
+         RemoteDMATransfer(dst_ids=[dst_id(topo, r) for r in near], dma_engine_mask=ON_CHIP, remote_sem=arrived,
+                           srcs=[buf], dsts=[buf for r in near])],
+        local_sem=T.sem.left)
+    g.wait_ge(T.sem.left, 16)
+
+
+def rank_store_program(g, T):
+    queues = [g.sync, g.scalar]
+    for k in range(NP):
+        q = queues[k % 2]
+        q.wait_ge(T.sem["a%d" % k], 8)
+        q.dma_start(rows_of(T.y, k), T["p%d" % k][:]).then_inc(T.sem.stored, 16)
+    g.wait_ge(T.sem.stored, 16 * NP)
 
 
 def rank_program(g, core, T, topo):
-    rank = T.rank_of(core)
-    if rank is None:
-        return
     if core == ROOT:
-        g.sync.dma_start(T.y[:], T.x[:]).then_inc(T.sem.stored, 16)
-        g.dma_start(T.land[:], T.x[:]).then_inc(T.sem.loaded, 16)
-        g.wait_ge(T.sem.loaded, 16)
-        _send(g, T, topo, [RELAY] + ODD)
-        g.wait_ge(T.sem.stored, 16)
+        root_program(g, T, topo)
         return
-    g.wait_ge(T.sem.arrived, 8)
-    g.sync.wait_ge(T.sem.arrived, 8)
-    g.sync.dma_start(T.y[:], T.land[:]).then_inc(T.sem.stored, 16)
-    if core == RELAY:
-        _send(g, T, topo, EVEN)
-    g.wait_ge(T.sem.stored, 16)
+    if T.rank_of(core) is not None:
+        rank_store_program(g, T)
+        return
+    for k in range(NP):
+        if PIECES[k][0] == core:
+            forwarder_program(g, core, k, T, topo)

from concourse.bass import DstId, RemoteDMATransfer

ROOT = 110
ROW = 1024
PIECES = [
    (15, 11), (7, 8),
    (31, 11), (23, 8),
    (127, 11), (119, 8),
    (123, 11), (3, 8),
    (11, 10), (19, 8),
    (27, 10), (115, 8),
    (98, 8), (99, 8),
]
NP = len(PIECES)
START = [sum(r for (c, r) in PIECES[:k]) for k in range(NP)]

SCRATCH = {"p%d" % k: ("dram", [128, PIECES[k][1] * ROW // 128], "float32") for k in range(NP)}
SEMAPHORES = ["a%d" % k for k in range(NP)] + ["left", "stored"]

OFF_CHIP = 0x00FF
ON_CHIP = 0xFF00


def dst_id(topo, core):
    rid, pid, sengine = topo.addr(core)
    return DstId(rid=rid, pnc=pid)


def rows_of(t, k):
    return t[START[k]:START[k] + PIECES[k][1], :]


def root_program(g, T, topo):
    queues = [g.sync, g.scalar]
    for k in range(NP):
        queues[k % 2].dma_start(T["p%d" % k][:], rows_of(T.x, k)).then_inc(T.sem["a%d" % k], 16)
    for k in range(NP):
        rid, pid, sengine = topo.addr(PIECES[k][0])
        g.wait_ge(T.sem["a%d" % k], 16)
        g.remote_dma(T["p%d" % k][:], T["p%d" % k][:], T.sem["a%d" % k], T.sem.left, pid, rid, OFF_CHIP)
    g.sync.wait_ge(T.sem.left, 8 * NP)
    g.sync.dma_start(T.y[:], T.x[:]).then_inc(T.sem.stored, 16)
    g.wait_ge(T.sem.stored, 16)


def forwarder_program(g, core, k, T, topo):
    buf = T["p%d" % k][:]
    arrived = T.sem["a%d" % k]
    far = [r for r in T.cores if r != ROOT and topo.chip(r) != topo.chip(core)]
    near = [r for r in T.cores if topo.chip(r) == topo.chip(core)]
    g.wait_ge(arrived, 8)
    g.remote_dma_fused(
        [RemoteDMATransfer(dst_ids=[dst_id(topo, r) for r in far], dma_engine_mask=OFF_CHIP, remote_sem=arrived,
                           srcs=[buf], dsts=[buf for r in far]),
         RemoteDMATransfer(dst_ids=[dst_id(topo, r) for r in near], dma_engine_mask=ON_CHIP, remote_sem=arrived,
                           srcs=[buf], dsts=[buf for r in near])],
        local_sem=T.sem.left)
    g.wait_ge(T.sem.left, 16)


def rank_store_program(g, T):
    queues = [g.sync, g.scalar]
    for k in range(NP):
        q = queues[k % 2]
        q.wait_ge(T.sem["a%d" % k], 8)
        q.dma_start(rows_of(T.y, k), T["p%d" % k][:]).then_inc(T.sem.stored, 16)
    g.wait_ge(T.sem.stored, 16 * NP)


def rank_program(g, core, T, topo):
    if core == ROOT:
        root_program(g, T, topo)
        return
    if T.rank_of(core) is not None:
        rank_store_program(g, T)
        return
    for k in range(NP):
        if PIECES[k][0] == core:
            forwarder_program(g, core, k, T, topo)
